import numpy as np
import ml_dtypes


def mxq(x, axis, fmt="e4m3"):
    dtype, down = {"e4m3": (ml_dtypes.float8_e4m3fn, 7), "e5m2": (ml_dtypes.float8_e5m2, 14)}[fmt]
    v = np.moveaxis(np.asarray(x, np.float32).astype(ml_dtypes.bfloat16).astype(np.float64), axis, -1)
    blocks = v.reshape(v.shape[:-1] + (-1, 32))
    amax = np.abs(blocks).max(-1, keepdims=True)
    byte = np.maximum(np.where(amax > 0, np.frexp(amax)[1] - 1 + 127, 0) - down, 1)
    scale = np.exp2(byte - 127.0)
    codes = (blocks / scale).astype(np.float32).astype(dtype).astype(np.float64)
    return np.moveaxis((codes * scale).reshape(v.shape), -1, axis)


WIDE = False


def mx_kscale(k):
    if not WIDE:
        return np.ones(k)
    levels = np.array([24, -24, 12, -12, 0])
    if k % 512:
        return np.exp2(np.random.permutation(np.resize(levels, k // 32))).repeat(32)
    a = np.empty((k // 512, 16))
    for p in range(k // 512):
        a[p, :8] = np.random.permutation(np.resize(levels, 8))
        for g in range(8):
            far = levels[np.abs(levels - a[p, g]) >= 10]
            a[p, g + 8] = far[np.random.randint(len(far))]
    return np.exp2(a.ravel()).repeat(32)


def f64(x):
    return np.asarray(x).astype(np.float64)


E2M1 = np.array([0.0, 0.5, 1.0, 1.5, 2.0, 3.0, 4.0, 6.0, -0.0, -0.5, -1.0, -1.5, -2.0, -3.0, -4.0, -6.0])


def pack_weight(w, fmt):
    k, n = w.shape
    w = f64(np.asarray(w, np.float32).astype(ml_dtypes.bfloat16)).reshape(k // 32, 32, n)
    amax = np.abs(w).max(1)
    if fmt == "e4m3":
        byte = np.frexp(amax)[1] - 1 + 127 - 7
    else:
        mant, ex = np.frexp(amax / 6.0)
        byte = np.where(mant > 0.5, ex, ex - 1) + 127
    byte = np.clip(np.where(amax > 0, byte, 1), 1, 254)
    scaled = (w * np.exp2(127.0 - byte)[:, None, :]).reshape(k, n).astype(np.float32)
    by_word = np.ascontiguousarray(scaled.reshape(k // 512, 128, 4, n).transpose(0, 1, 3, 2))
    if fmt == "e4m3":
        words = by_word.astype(ml_dtypes.float8_e4m3fn).view(np.uint8)
    else:
        c = by_word.astype(ml_dtypes.float4_e2m1fn).view(np.uint8) & 0xF
        words = (c[..., 0::2] | (c[..., 1::2] << 4)).reshape(k // 512, 128, 2 * n)
    return np.ascontiguousarray(words), np.ascontiguousarray(byte.astype(np.uint8).reshape(k // 512, 16, n))


def unpack_weight(words, scales, fmt):
    g, _, n = scales.shape
    words = np.ascontiguousarray(words).reshape(g, 128, n, -1)
    if fmt == "e4m3":
        vals = words.view(ml_dtypes.float8_e4m3fn).astype(np.float64)
    else:
        nib = np.empty((g, 128, n, 4), np.uint8)
        nib[..., 0::2] = words & 0xF
        nib[..., 1::2] = words >> 4
        vals = E2M1[nib]
    vals = vals * np.repeat(np.exp2(scales.astype(np.float64) - 127.0), 8, axis=1)[..., None]
    return vals.transpose(0, 1, 3, 2).reshape(g * 512, n)


def planes(y):
    n, m = y.shape
    v = y.astype(np.float32).astype(ml_dtypes.bfloat16).astype(np.float64).reshape(n // 32, 32, m)
    top = np.abs(v).max(1)
    byte = np.clip(np.where(top > 0, np.frexp(top)[1] - 1 + 127 - 7, 1), 1, 254)
    codes = (v * np.exp2(127.0 - byte)[:, None, :]).reshape(n, m).astype(np.float32).astype(ml_dtypes.float8_e4m3fn).view(np.uint8)
    words = codes.reshape(n // 512, 128, 4, m).transpose(0, 1, 3, 2)
    return np.ascontiguousarray(words), np.ascontiguousarray(byte.astype(np.uint8).reshape(n // 512, 16, m))


def sigm(f):
    return 1.0 / (1.0 + np.exp(-np.maximum(f, -700.0)))


K, N, T, M = 512, 1024, 1024, 1024


def setup_inputs():
    n = np.random.standard_normal
    s = mx_kscale(K)[:, None]
    s2 = mx_kscale(N)[:, None]
    h = np.tanh(n((N, T)))
    p_hq = pack_weight(h * s2, "e4m3")
    p_wz = pack_weight(n((K, N)) / np.sqrt(K) / s, "e2m1")
    p_uz = pack_weight(n((N, N)) / np.sqrt(N) / s2, "e4m3")
    p_wn = pack_weight(n((K, N)) / np.sqrt(K) / s, "e2m1")
    p_un = pack_weight(n((N, N)) / np.sqrt(N) / s2, "e4m3")
    return {
        "x": (n((K, T)) * s).astype(np.float32),
        "hq_words": p_hq[0],
        "hq_scales": p_hq[1],
        "wz_words": p_wz[0],
        "wz_scales": p_wz[1],
        "uz_words": p_uz[0],
        "uz_scales": p_uz[1],
        "wn_words": p_wn[0],
        "wn_scales": p_wn[1],
        "un_words": p_un[0],
        "un_scales": p_un[1],
        "bz": (0.3 * n(N)).astype(np.float32),
        "bn": (0.3 * n(N)).astype(np.float32),
        "h": (h).astype(np.float32),
    }


def reference(x, hq_words, hq_scales, wz_words, wz_scales, uz_words, uz_scales, wn_words, wn_scales, un_words, un_scales, bz, bn, h):
    x_ = mxq(f64(x), 0, "e4m3")
    hq_ = unpack_weight(hq_words, hq_scales, "e4m3")
    wz_ = unpack_weight(wz_words, wz_scales, "e2m1")
    uz_ = unpack_weight(uz_words, uz_scales, "e4m3")
    wn_ = unpack_weight(wn_words, wn_scales, "e2m1")
    un_ = unpack_weight(un_words, un_scales, "e4m3")
    sz = wz_.T @ x_ + uz_.T @ hq_
    z = sigm(sz + f64(bz)[:, None])
    xn = wn_.T @ x_
    hn = un_.T @ hq_
    c = np.tanh(xn + f64(bn)[:, None] + z * hn)
    out_0 = f64(h) + z * (c - f64(h))
    return (out_0,) + planes(out_0)

@@ -1,0 +1,324 @@
+from contextlib import ExitStack
+
+import concourse.mybir as mybir
+
+K, N, T = 512, 1024, 1024
+FLOPS = 2 * T * N * (2 * K + 2 * N)
+
+F32 = mybir.dt.float32
+BF16 = mybir.dt.bfloat16
+I32 = mybir.dt.int32
+U32 = mybir.dt.uint32
+U8 = mybir.dt.uint8
+FP8X4 = mybir.dt.float8_e4m3fn_x4
+FP4X4 = mybir.dt.float4_e2m1fn_x4
+ACT = mybir.ActivationFunctionType
+ALU = mybir.AluOpType
+
+P = 128
+PACK = 4
+ROWS = P * PACK
+W = 256
+HALF = W // 2
+CHUNKS = T // W
+UNITS = (N // ROWS) * CHUNKS
+
+
+def tile_mix_gru_mgu_kernel(
+    tc, x, hq_words, hq_scales, wz_words, wz_scales, uz_words, uz_scales,
+    wn_words, wn_scales, un_words, un_scales, bz, bn, h, out_0, out_1, out_2,
+):
+    nc = tc.nc
+    with ExitStack() as ctx:
+        keep = ctx.enter_context(tc.tile_pool(name="keep", bufs=1))
+        work = ctx.enter_context(tc.tile_pool(name="work", bufs=2))
+        psum = ctx.enter_context(tc.psum_pool(name="psum", bufs=2))
+        ctx.enter_context(tc.manual_schedule())
+
+        def kept(name, shape, dtype):
+            return keep.tile(shape, dtype, name=name, align_bytes=64)
+
+        x_raw = [kept("x_raw%d" % c, [P, PACK, W], F32) for c in range(CHUNKS)]
+        x_codes = kept("x_codes", [P, T], U32)
+        x_plane = kept("x_plane", [P, T], U8)
+        hq_codes = [kept("hq_codes%d" % c, [P, 2, W], U32) for c in range(CHUNKS)]
+        hq_plane = kept("hq_plane", [P, 2, T], U8)
+        h_sb = [kept("h_sb%d" % u, [P, PACK, W], F32) for u in range(UNITS)]
+        o_sb = [kept("o_sb%d" % u, [P, PACK, W], F32) for u in range(UNITS)]
+        o_codes = [kept("o_codes%d" % a, [P, T], U32) for a in range(2)]
+        o_plane = kept("o_plane", [P, 2, T], U8)
+        gates = ("z", "n")
+        w_words = {"z": wz_words, "n": wn_words}
+        w_scales = {"z": wz_scales, "n": wn_scales}
+        u_words = {"z": uz_words, "n": un_words}
+        u_scales = {"z": uz_scales, "n": un_scales}
+        bias_hbm = {"z": bz, "n": bn}
+        bias = {g: kept("bias_" + g, [P, 2, PACK], F32) for g in gates}
+        s_raw = {g: kept("s_raw_" + g, [P, N], U8) for g in gates}
+        u_raw, u_dealt, w_raw, w_dealt, s_dealt = {}, {}, {}, {}, {}
+        for g in gates:
+            for a in range(2):
+                u_raw[g, a] = kept("u_raw_%s%d" % (g, a), [P, 2, ROWS], U32)
+                u_dealt[g, a] = kept("u_dealt_%s%d" % (g, a), [P, 2, ROWS], U32)
+                w_raw[g, a] = kept("w_raw_%s%d" % (g, a), [P, 2 * ROWS], U8)
+                w_dealt[g, a] = kept("w_dealt_%s%d" % (g, a), [P, 2 * ROWS], U8)
+                s_dealt[g, a] = kept("s_dealt_%s%d" % (g, a), [P, ROWS], U8)
+
+        def unit_rows(ap, u):
+            a, c = divmod(u, CHUNKS)
+            return ap[a * ROWS:(a + 1) * ROWS, c * W:(c + 1) * W].rearrange("(p r) t -> p r t", r=PACK)
+
+        def load_x(c):
+            nc.sync.dma_start(out=x_raw[c][:], in_=x[:, c * W:(c + 1) * W].rearrange("(p j) t -> p j t", j=PACK))
+
+        def load_hq(c):
+            src = hq_words.rearrange("g p t i -> p g (t i)")[:, :, 4 * c * W:4 * (c + 1) * W]
+            nc.sync.dma_start(out=hq_codes[c][:].bitcast(I32), in_=src.bitcast(I32))
+
+        def load_u(g, a):
+            src = u_words[g].rearrange("g p n i -> p g (n i)")[:, :, 4 * a * ROWS:4 * (a + 1) * ROWS]
+            nc.sync.dma_start(out=u_raw[g, a][:].bitcast(I32), in_=src.bitcast(I32))
+
+        def load_w(g, a):
+            src = w_words[g][0][:, 2 * a * ROWS:2 * (a + 1) * ROWS]
+            nc.sync.dma_start(out=w_raw[g, a][:].bitcast(I32), in_=src.bitcast(I32))
+
+        def load_h(u):
+            nc.sync.dma_start(out=h_sb[u][:], in_=unit_rows(h, u))
+
+        def load_w_scales(eng, g, q):
+            eng.dma_start(out=s_raw[g][32 * q:32 * q + 4, :].bitcast(I32),
+                          in_=w_scales[g][0][4 * q:4 * q + 4, :].bitcast(I32))
+
+        def load_u_scales(eng, g, q):
+            eng.dma_start(out=s_raw[g][32 * q + 4:32 * q + 12, :].bitcast(I32),
+                          in_=u_scales[g][:, 4 * q:4 * q + 4, :].bitcast(I32))
+
+        def load_hq_scales(eng, q):
+            eng.dma_start(out=hq_plane[32 * q:32 * q + 4, :, :].bitcast(I32),
+                          in_=hq_scales[:, 4 * q:4 * q + 4, :].rearrange("g r t -> r g t").bitcast(I32))
+
+        def load_bias(eng, g):
+            eng.dma_start(out=bias[g][:], in_=bias_hbm[g].rearrange("(a p r) -> p a r", a=2, r=PACK))
+
+        def deal_u(g, a):
+            nc.vector.tensor_copy(
+                out=u_dealt[g, a][:].bitcast(I32).rearrange("p g (r b i) -> p g b r i", r=PACK, i=4),
+                in_=u_raw[g, a][:].bitcast(I32).rearrange("p g (b i r) -> p g b r i", r=PACK, i=4))
+
+        def deal_w(g, a):
+            nc.vector.tensor_copy(
+                out=w_dealt[g, a][:].rearrange("p (r b i y) -> p b r i y", r=PACK, i=8, y=2),
+                in_=w_raw[g, a][:].rearrange("p (b i r y) -> p b r i y", r=PACK, i=8, y=2))
+
+        def deal_s(g, a):
+            nc.vector.tensor_copy(
+                out=s_dealt[g, a][:].rearrange("p (r b i) -> p b r i", r=PACK, i=16),
+                in_=s_raw[g][:, a * ROWS:(a + 1) * ROWS].rearrange("p (b i r) -> p b r i", r=PACK, i=16))
+
+        def interleave(src, tag):
+            width = src.shape[2]
+            dst = work.tile([P, PACK * W], BF16, name=tag, tag=tag, bufs=3, align_bytes=64)
+            nc.scalar.copy(
+                out=dst[:, :PACK * width].rearrange("p (c i j) -> p c j i", i=4, j=PACK),
+                in_=src.rearrange("p j (c i) -> p c j i", i=4))
+            return dst[:, :PACK * width]
+
+        def quantize(codes, plane, src):
+            nc.vector.quantize_mx(out=codes.bitcast(FP8X4), scales=plane, in_=src)
+
+        def quantize_x(c, src):
+            quantize(x_codes[:, c * W:(c + 1) * W], x_plane[:, c * W:(c + 1) * W], src)
+
+        def quantize_o(u, t0, width, src):
+            a, c = divmod(u, CHUNKS)
+            cols = slice(c * W + t0, c * W + t0 + width)
+            quantize(o_codes[a][:, cols], o_plane[:, a, cols], src)
+
+        def pieces(u, b):
+            if u == UNITS - 1:
+                return [(r, b * HALF, HALF) for r in range(PACK)]
+            return [(r, 0, W) for r in (2 * b, 2 * b + 1)]
+
+        def part(tile, u, b):
+            if u == UNITS - 1:
+                return tile[:, :, b * HALF:(b + 1) * HALF]
+            return tile[:, 2 * b:2 * b + 2, :]
+
+        def bank_view(bank, u):
+            return bank[:].rearrange("p (r t) -> p r t", t=HALF if u == UNITS - 1 else W)
+
+        def u_pass(dst, g, u, r, t0, width, j, start, stop):
+            a, c = divmod(u, CHUNKS)
+            cols = slice(r * P, (r + 1) * P)
+            nc.tensor.matmul_mx(
+                out=dst, lhsT=u_dealt[g, a][:, j, cols].bitcast(FP8X4),
+                lhsT_scale=s_dealt[g, a][4 * (j + 1):P, cols],
+                rhs=hq_codes[c][:, j, t0:t0 + width].bitcast(FP8X4),
+                rhs_scale=hq_plane[:, j, c * W + t0:c * W + t0 + width], start=start, stop=stop)
+
+        def w_pass(dst, g, u, r, t0, width, start, stop):
+            a, c = divmod(u, CHUNKS)
+            cols = slice(c * W + t0, c * W + t0 + width)
+            nc.tensor.matmul_mx(
+                out=dst, lhsT=w_dealt[g, a][:, 2 * r * P:2 * (r + 1) * P].bitcast(FP4X4),
+                lhsT_scale=s_dealt[g, a][:, r * P:(r + 1) * P],
+                rhs=x_codes[:, cols].bitcast(FP8X4), rhs_scale=x_plane[:, cols], start=start, stop=stop)
+
+        sz, hn, xn, z, y, cand = {}, {}, {}, {}, {}, {}
+
+        def mm_sz(u):
+            for b in range(2):
+                sz[u, b] = psum.tile([P, 512], F32, name="sz", tag="sz", bufs=2)
+                for i, (r, t0, width) in enumerate(pieces(u, b)):
+                    for s in range(0, width, HALF):
+                        dst = sz[u, b][:, i * width + s:i * width + s + HALF]
+                        u_pass(dst, "z", u, r, t0 + s, HALF, 0, True, False)
+                        u_pass(dst, "z", u, r, t0 + s, HALF, 1, False, False)
+                        w_pass(dst, "z", u, r, t0 + s, HALF, False, True)
+
+        def mm_hn(u):
+            for b in range(2):
+                hn[u, b] = psum.tile([P, 512], F32, name="hn", tag="hn", bufs=3)
+                for i, (r, t0, width) in enumerate(pieces(u, b)):
+                    dst = hn[u, b][:, i * width:(i + 1) * width]
+                    u_pass(dst, "n", u, r, t0, width, 0, True, False)
+                    u_pass(dst, "n", u, r, t0, width, 1, False, True)
+
+        def mm_xn(u):
+            for b in range(2):
+                xn[u, b] = psum.tile([P, 512], F32, name="xn", tag="xn", bufs=3)
+                for i, (r, t0, width) in enumerate(pieces(u, b)):
+                    w_pass(xn[u, b][:, i * width:(i + 1) * width], "n", u, r, t0, width, True, True)
+
+        def gate(u):
+            z[u] = work.tile([P, PACK, W], F32, name="z", tag="z", bufs=3)
+            for b in range(2):
+                for i, (r, t0, width) in enumerate(pieces(u, b)):
+                    nc.scalar.activation(out=z[u][:, r, t0:t0 + width], in_=sz[u, b][:, i * width:(i + 1) * width],
+                                         func=ACT.Sigmoid, bias=bias["z"][:, u // CHUNKS, r:r + 1])
+
+        def preact(u):
+            y[u] = work.tile([P, PACK, W], F32, name="y", tag="y", bufs=2)
+            for b in range(2):
+                nc.vector.tensor_tensor(out=part(y[u], u, b), in0=bank_view(hn[u, b], u), in1=part(z[u], u, b), op=ALU.mult)
+            for b in range(2):
+                nc.vector.tensor_tensor(out=part(y[u], u, b), in0=bank_view(xn[u, b], u), in1=part(y[u], u, b), op=ALU.add)
+
+        def candidate(u):
+            cand[u] = work.tile([P, PACK, W], F32, name="cand", tag="cand", bufs=3)
+            for b in range(2):
+                for r, t0, width in pieces(u, b):
+                    nc.scalar.activation(out=cand[u][:, r, t0:t0 + width], in_=y[u][:, r, t0:t0 + width],
+                                         func=ACT.Tanh, bias=bias["n"][:, u // CHUNKS, r:r + 1])
+
+        def step(u):
+            for b in range(2):
+                nc.vector.tensor_tensor(out=part(cand[u], u, b), in0=part(cand[u], u, b), in1=part(h_sb[u], u, b), op=ALU.subtract)
+            for b in range(2):
+                nc.vector.tensor_tensor(out=part(cand[u], u, b), in0=part(cand[u], u, b), in1=part(z[u], u, b), op=ALU.mult)
+
+        def store_out(u):
+            nc.sync.dma_start(out=unit_rows(out_0, u), in_=o_sb[u][:])
+
+        def store_codes(a, t0, t1):
+            nc.sync.dma_start(out=out_1[a].rearrange("p t i -> p (t i)")[:, 4 * t0:4 * t1].bitcast(I32),
+                              in_=o_codes[a][:, t0:t1].bitcast(I32))
+
+        nc.vector.memset(s_raw["z"][:].bitcast(I32), 0)
+        nc.vector.memset(s_raw["n"][:].bitcast(I32), 0)
+        nc.vector.memset(hq_plane[:].bitcast(I32), 0)
+        load_x(0)
+        load_u("z", 0)
+        for q in range(4):
+            load_u_scales(nc.sync, "z", q)
+        for q in range(2):
+            load_w_scales(nc.sync, "z", q)
+        load_u("n", 0)
+        load_hq(0)
+        for q in range(2, 4):
+            load_w_scales(nc.sync, "z", q)
+        for q in range(4):
+            load_hq_scales(nc.sync, q)
+        load_w("z", 0)
+        load_w("n", 0)
+        for q in range(4):
+            load_w_scales(nc.sync, "n", q)
+        for q in range(4):
+            load_u_scales(nc.gpsimd, "n", q)
+        load_bias(nc.gpsimd, "z")
+        load_bias(nc.gpsimd, "n")
+        load_x(1)
+        load_hq(1)
+        load_h(0)
+        load_u("z", 1)
+        load_x(2)
+        load_hq(2)
+        load_h(1)
+        load_u("n", 1)
+        load_w("z", 1)
+        load_w("n", 1)
+        load_x(3)
+        load_hq(3)
+        for u in range(2, UNITS):
+            load_h(u)
+
+        x_bf = interleave(x_raw[0][:], "x_bf")
+        deal_u("z", 0)
+        quantize_x(0, x_bf)
+        deal_u("n", 0)
+        deal_s("z", 0)
+        deal_w("z", 0)
+        deal_s("n", 0)
+        deal_w("n", 0)
+        deal_s("z", 1)
+        deal_s("n", 1)
+        mm_sz(0)
+        mm_hn(0)
+        mm_xn(0)
+        gate(0)
+
+        later_deals = {0: [(deal_u, "z")], 1: [(deal_u, "n"), (deal_w, "z")], 2: [(deal_w, "n")]}
+        o_bf = {}
+        for u in range(UNITS):
+            nxt = u + 1
+            if nxt < CHUNKS:
+                x_bf = interleave(x_raw[nxt][:], "x_bf")
+            preact(u)
+            if u >= 1:
+                nc.gpsimd.tensor_tensor(out=o_sb[u - 1][:], in0=cand[u - 1][:], in1=h_sb[u - 1][:], op=ALU.add)
+                store_out(u - 1)
+            if nxt < CHUNKS:
+                quantize_x(nxt, x_bf)
+            if u >= 2:
+                quantize_o(u - 2, 0, W, o_bf[u - 2])
+                if u - 2 == CHUNKS - 1:
+                    store_codes(0, 0, T)
+            for fn, g in later_deals.get(u, []):
+                fn(g, 1)
+            candidate(u)
+            if nxt < UNITS:
+                mm_hn(nxt)
+                mm_sz(nxt)
+                mm_xn(nxt)
+                gate(nxt)
+            if u >= 1:
+                o_bf[u - 1] = interleave(o_sb[u - 1][:], "o_bf")
+            step(u)
+
+        last = UNITS - 1
+        tail = []
+        for b in range(2):
+            nc.vector.tensor_tensor(out=part(o_sb[last], last, b), in0=part(cand[last], last, b),
+                                    in1=part(h_sb[last], last, b), op=ALU.add)
+            tail.append(interleave(part(o_sb[last], last, b), "o_bf"))
+            if b == 0:
+                quantize_o(last - 1, 0, W, o_bf[last - 1])
+                store_codes(1, 0, T - W)
+        store_out(last)
+        for b in range(2):
+            quantize_o(last, b * HALF, HALF, tail[b])
+        store_codes(1, T - W, T)
+        for q in range(4):
+            nc.sync.dma_start(out=out_2[:, 4 * q:4 * q + 4, :].rearrange("a r t -> r a t").bitcast(I32),
+                              in_=o_plane[32 * q:32 * q + 4, :, :].bitcast(I32))

@@ -118,7 +118,7 @@ def tile_mix_gru_mgu_kernel(
 
         def interleave(src, tag):
             width = src.shape[2]
-            dst = work.tile([P, PACK * W], BF16, name=tag, tag=tag, bufs=3, align_bytes=64)
+            dst = work.tile([P, PACK * W], BF16, name=tag, tag=tag, bufs=4, align_bytes=64)
             nc.scalar.copy(
                 out=dst[:, :PACK * width].rearrange("p (c i j) -> p c j i", i=4, j=PACK),
                 in_=src.rearrange("p j (c i) -> p c j i", i=4))
@@ -167,29 +167,28 @@ def tile_mix_gru_mgu_kernel(
 
         sz, hn, xn, z, y, cand = {}, {}, {}, {}, {}, {}
 
-        def mm_sz(u):
-            for b in range(2):
-                sz[u, b] = psum.tile([P, 512], F32, name="sz", tag="sz", bufs=2)
-                for i, (r, t0, width) in enumerate(pieces(u, b)):
-                    for s in range(0, width, HALF):
-                        dst = sz[u, b][:, i * width + s:i * width + s + HALF]
-                        u_pass(dst, "z", u, r, t0 + s, HALF, 0, True, False)
-                        u_pass(dst, "z", u, r, t0 + s, HALF, 1, False, False)
-                        w_pass(dst, "z", u, r, t0 + s, HALF, False, True)
+        def mm_sz(u, b):
+            sz[u, b] = psum.tile([P, 512], F32, name="sz", tag="sz", bufs=2)
+            todo = list(enumerate(pieces(u, b)))
+            for i, (r, t0, width) in todo:
+                for j in range(2):
+                    u_pass(sz[u, b][:, i * width:(i + 1) * width], "z", u, r, t0, width, j, i == 0 and j == 0, False)
+            for i, (r, t0, width) in todo:
+                for s in range(0, width, HALF):
+                    col = i * width + s
+                    w_pass(sz[u, b][:, col:col + HALF], "z", u, r, t0 + s, HALF, False, col + HALF == 512)
 
-        def mm_hn(u):
-            for b in range(2):
-                hn[u, b] = psum.tile([P, 512], F32, name="hn", tag="hn", bufs=3)
-                for i, (r, t0, width) in enumerate(pieces(u, b)):
-                    dst = hn[u, b][:, i * width:(i + 1) * width]
-                    u_pass(dst, "n", u, r, t0, width, 0, True, False)
-                    u_pass(dst, "n", u, r, t0, width, 1, False, True)
+        def mm_hn(u, b):
+            hn[u, b] = psum.tile([P, 512], F32, name="hn", tag="hn", bufs=3)
+            for i, (r, t0, width) in enumerate(pieces(u, b)):
+                dst = hn[u, b][:, i * width:(i + 1) * width]
+                u_pass(dst, "n", u, r, t0, width, 0, True, False)
+                u_pass(dst, "n", u, r, t0, width, 1, False, True)
 
-        def mm_xn(u):
-            for b in range(2):
-                xn[u, b] = psum.tile([P, 512], F32, name="xn", tag="xn", bufs=3)
-                for i, (r, t0, width) in enumerate(pieces(u, b)):
-                    w_pass(xn[u, b][:, i * width:(i + 1) * width], "n", u, r, t0, width, True, True)
+        def mm_xn(u, b):
+            xn[u, b] = psum.tile([P, 512], F32, name="xn", tag="xn", bufs=3)
+            for i, (r, t0, width) in enumerate(pieces(u, b)):
+                w_pass(xn[u, b][:, i * width:(i + 1) * width], "n", u, r, t0, width, True, True)
 
         def gate(u):
             z[u] = work.tile([P, PACK, W], F32, name="z", tag="z", bufs=3)
@@ -198,10 +197,12 @@ def tile_mix_gru_mgu_kernel(
                     nc.scalar.activation(out=z[u][:, r, t0:t0 + width], in_=sz[u, b][:, i * width:(i + 1) * width],
                                          func=ACT.Sigmoid, bias=bias["z"][:, u // CHUNKS, r:r + 1])
 
+        def gated(u, b):
+            if b == 0:
+                y[u] = work.tile([P, PACK, W], F32, name="y", tag="y", bufs=2)
+            nc.vector.tensor_tensor(out=part(y[u], u, b), in0=bank_view(hn[u, b], u), in1=part(z[u], u, b), op=ALU.mult)
+
         def preact(u):
-            y[u] = work.tile([P, PACK, W], F32, name="y", tag="y", bufs=2)
-            for b in range(2):
-                nc.vector.tensor_tensor(out=part(y[u], u, b), in0=bank_view(hn[u, b], u), in1=part(z[u], u, b), op=ALU.mult)
             for b in range(2):
                 nc.vector.tensor_tensor(out=part(y[u], u, b), in0=bank_view(xn[u, b], u), in1=part(y[u], u, b), op=ALU.add)
 
@@ -218,44 +219,46 @@ def tile_mix_gru_mgu_kernel(
             for b in range(2):
                 nc.vector.tensor_tensor(out=part(cand[u], u, b), in0=part(cand[u], u, b), in1=part(z[u], u, b), op=ALU.mult)
 
-        def store_out(u):
-            nc.sync.dma_start(out=unit_rows(out_0, u), in_=o_sb[u][:])
+        def store_out(u, t0, t1):
+            nc.sync.dma_start(out=unit_rows(out_0, u)[:, :, t0:t1], in_=o_sb[u][:, :, t0:t1])
 
         def store_codes(a, t0, t1):
             nc.sync.dma_start(out=out_1[a].rearrange("p t i -> p (t i)")[:, 4 * t0:4 * t1].bitcast(I32),
                               in_=o_codes[a][:, t0:t1].bitcast(I32))
 
         nc.vector.memset(s_raw["z"][:].bitcast(I32), 0)
-        nc.vector.memset(s_raw["n"][:].bitcast(I32), 0)
         nc.vector.memset(hq_plane[:].bitcast(I32), 0)
-        load_x(0)
+        nc.vector.memset(s_raw["n"][:].bitcast(I32), 0)
         load_u("z", 0)
+        load_x(0)
         for q in range(4):
             load_u_scales(nc.sync, "z", q)
         for q in range(2):
             load_w_scales(nc.sync, "z", q)
-        load_u("n", 0)
         load_hq(0)
+        load_w("z", 0)
         for q in range(2, 4):
             load_w_scales(nc.sync, "z", q)
         for q in range(4):
             load_hq_scales(nc.sync, q)
-        load_w("z", 0)
+        load_u("n", 0)
         load_w("n", 0)
         for q in range(4):
+            load_u_scales(nc.sync, "n", q)
+        for q in range(2):
             load_w_scales(nc.sync, "n", q)
-        for q in range(4):
-            load_u_scales(nc.gpsimd, "n", q)
+        for q in range(2, 4):
+            load_w_scales(nc.gpsimd, "n", q)
         load_bias(nc.gpsimd, "z")
         load_bias(nc.gpsimd, "n")
         load_x(1)
         load_hq(1)
-        load_h(0)
         load_u("z", 1)
+        load_h(0)
         load_x(2)
         load_hq(2)
-        load_h(1)
         load_u("n", 1)
+        load_h(1)
         load_w("z", 1)
         load_w("n", 1)
         load_x(3)
@@ -265,42 +268,49 @@ def tile_mix_gru_mgu_kernel(
 
         x_bf = interleave(x_raw[0][:], "x_bf")
         deal_u("z", 0)
-        quantize_x(0, x_bf)
-        deal_u("n", 0)
-        deal_s("z", 0)
         deal_w("z", 0)
+        quantize_x(0, x_bf)
+        deal_s("z", 0)
+        deal_u("n", 0)
         deal_s("n", 0)
         deal_w("n", 0)
-        deal_s("z", 1)
-        deal_s("n", 1)
-        mm_sz(0)
-        mm_hn(0)
-        mm_xn(0)
+        for b in range(2):
+            mm_sz(0, b)
+            mm_hn(0, b)
+        for b in range(2):
+            mm_xn(0, b)
         gate(0)
 
-        later_deals = {0: [(deal_u, "z")], 1: [(deal_u, "n"), (deal_w, "z")], 2: [(deal_w, "n")]}
+        later_deals = {0: [(deal_u, "z")], 1: [(deal_u, "n")], 2: [(deal_w, "z"), (deal_w, "n")]}
         o_bf = {}
         for u in range(UNITS):
             nxt = u + 1
             if nxt < CHUNKS:
                 x_bf = interleave(x_raw[nxt][:], "x_bf")
+            gated(u, 0)
+            if u == 0:
+                deal_s("z", 1)
+                deal_s("n", 1)
+            gated(u, 1)
             preact(u)
             if u >= 1:
                 nc.gpsimd.tensor_tensor(out=o_sb[u - 1][:], in0=cand[u - 1][:], in1=h_sb[u - 1][:], op=ALU.add)
-                store_out(u - 1)
+                store_out(u - 1, 0, W)
             if nxt < CHUNKS:
                 quantize_x(nxt, x_bf)
             if u >= 2:
                 quantize_o(u - 2, 0, W, o_bf[u - 2])
                 if u - 2 == CHUNKS - 1:
                     store_codes(0, 0, T)
+                if u == UNITS - 1:
+                    store_codes(1, 0, T - 2 * W)
             for fn, g in later_deals.get(u, []):
                 fn(g, 1)
             candidate(u)
             if nxt < UNITS:
-                mm_hn(nxt)
-                mm_sz(nxt)
-                mm_xn(nxt)
+                for mm in (mm_hn, mm_sz, mm_xn):
+                    for b in range(2):
+                        mm(nxt, b)
                 gate(nxt)
             if u >= 1:
                 o_bf[u - 1] = interleave(o_sb[u - 1][:], "o_bf")
@@ -312,13 +322,11 @@ def tile_mix_gru_mgu_kernel(
             nc.vector.tensor_tensor(out=part(o_sb[last], last, b), in0=part(cand[last], last, b),
                                     in1=part(h_sb[last], last, b), op=ALU.add)
             tail.append(interleave(part(o_sb[last], last, b), "o_bf"))
-            if b == 0:
-                quantize_o(last - 1, 0, W, o_bf[last - 1])
-                store_codes(1, 0, T - W)
-        store_out(last)
+            store_out(last, b * HALF, (b + 1) * HALF)
+        quantize_o(last - 1, 0, W, o_bf[last - 1])
         for b in range(2):
             quantize_o(last, b * HALF, HALF, tail[b])
-        store_codes(1, T - W, T)
+        store_codes(1, T - 2 * W, T)
         for q in range(4):
             nc.sync.dma_start(out=out_2[:, 4 * q:4 * q + 4, :].rearrange("a r t -> r a t").bitcast(I32),
                               in_=o_plane[32 * q:32 * q + 4, :, :].bitcast(I32))

@@ -45,7 +45,7 @@ def tile_mix_gru_mgu_kernel(
         hq_plane = kept("hq_plane", [P, 2, T], U8)
         h_sb = [kept("h_sb%d" % u, [P, PACK, W], F32) for u in range(UNITS)]
         o_sb = [kept("o_sb%d" % u, [P, PACK, W], F32) for u in range(UNITS)]
-        o_codes = [kept("o_codes%d" % a, [P, T], U32) for a in range(2)]
+        o_codes = kept("o_codes", [P, 2, T], U32)
         o_plane = kept("o_plane", [P, 2, T], U8)
         gates = ("z", "n")
         w_words = {"z": wz_words, "n": wn_words}
@@ -65,7 +65,7 @@ def tile_mix_gru_mgu_kernel(
                 s_dealt[g, a] = kept("s_dealt_%s%d" % (g, a), [P, ROWS], U8)
 
         def unit_rows(ap, u):
-            a, c = divmod(u, CHUNKS)
+            c, a = divmod(u, 2)
             return ap[a * ROWS:(a + 1) * ROWS, c * W:(c + 1) * W].rearrange("(p r) t -> p r t", r=PACK)
 
         def load_x(c):
@@ -116,24 +116,24 @@ def tile_mix_gru_mgu_kernel(
                 out=s_dealt[g, a][:].rearrange("p (r b i) -> p b r i", r=PACK, i=16),
                 in_=s_raw[g][:, a * ROWS:(a + 1) * ROWS].rearrange("p (b i r) -> p b r i", r=PACK, i=16))
 
-        def interleave(src, tag):
-            width = src.shape[2]
-            dst = work.tile([P, PACK * W], BF16, name=tag, tag=tag, bufs=4, align_bytes=64)
+        def bf_tile(tag):
+            return work.tile([P, PACK * W], BF16, name=tag, tag=tag, bufs=3, align_bytes=64)
+
+        def interleave(dst, src, t0, t1):
             nc.scalar.copy(
-                out=dst[:, :PACK * width].rearrange("p (c i j) -> p c j i", i=4, j=PACK),
-                in_=src.rearrange("p j (c i) -> p c j i", i=4))
-            return dst[:, :PACK * width]
+                out=dst[:, PACK * t0:PACK * t1].rearrange("p (c i j) -> p c j i", i=2, j=PACK),
+                in_=src[:, :, t0:t1].rearrange("p j (c i) -> p c j i", i=2))
 
         def quantize(codes, plane, src):
             nc.vector.quantize_mx(out=codes.bitcast(FP8X4), scales=plane, in_=src)
 
         def quantize_x(c, src):
-            quantize(x_codes[:, c * W:(c + 1) * W], x_plane[:, c * W:(c + 1) * W], src)
+            quantize(x_codes[:, c * W:(c + 1) * W], x_plane[:, c * W:(c + 1) * W], src[:])
 
         def quantize_o(u, t0, width, src):
-            a, c = divmod(u, CHUNKS)
+            c, a = divmod(u, 2)
             cols = slice(c * W + t0, c * W + t0 + width)
-            quantize(o_codes[a][:, cols], o_plane[:, a, cols], src)
+            quantize(o_codes[:, a, cols], o_plane[:, a, cols], src[:, PACK * t0:PACK * (t0 + width)])
 
         def pieces(u, b):
             if u == UNITS - 1:
@@ -149,7 +149,7 @@ def tile_mix_gru_mgu_kernel(
             return bank[:].rearrange("p (r t) -> p r t", t=HALF if u == UNITS - 1 else W)
 
         def u_pass(dst, g, u, r, t0, width, j, start, stop):
-            a, c = divmod(u, CHUNKS)
+            c, a = divmod(u, 2)
             cols = slice(r * P, (r + 1) * P)
             nc.tensor.matmul_mx(
                 out=dst, lhsT=u_dealt[g, a][:, j, cols].bitcast(FP8X4),
@@ -158,7 +158,7 @@ def tile_mix_gru_mgu_kernel(
                 rhs_scale=hq_plane[:, j, c * W + t0:c * W + t0 + width], start=start, stop=stop)
 
         def w_pass(dst, g, u, r, t0, width, start, stop):
-            a, c = divmod(u, CHUNKS)
+            c, a = divmod(u, 2)
             cols = slice(c * W + t0, c * W + t0 + width)
             nc.tensor.matmul_mx(
                 out=dst, lhsT=w_dealt[g, a][:, 2 * r * P:2 * (r + 1) * P].bitcast(FP4X4),
@@ -168,7 +168,7 @@ def tile_mix_gru_mgu_kernel(
         sz, hn, xn, z, y, cand = {}, {}, {}, {}, {}, {}
 
         def mm_sz(u, b):
-            sz[u, b] = psum.tile([P, 512], F32, name="sz", tag="sz", bufs=2)
+            sz[u, b] = psum.tile([P, 512], F32, name="sz", tag="sz", bufs=3)
             todo = list(enumerate(pieces(u, b)))
             for i, (r, t0, width) in todo:
                 for j in range(2):
@@ -179,7 +179,7 @@ def tile_mix_gru_mgu_kernel(
                     w_pass(sz[u, b][:, col:col + HALF], "z", u, r, t0 + s, HALF, False, col + HALF == 512)
 
         def mm_hn(u, b):
-            hn[u, b] = psum.tile([P, 512], F32, name="hn", tag="hn", bufs=3)
+            hn[u, b] = psum.tile([P, 512], F32, name="hn", tag="hn", bufs=2)
             for i, (r, t0, width) in enumerate(pieces(u, b)):
                 dst = hn[u, b][:, i * width:(i + 1) * width]
                 u_pass(dst, "n", u, r, t0, width, 0, True, False)
@@ -195,7 +195,7 @@ def tile_mix_gru_mgu_kernel(
             for b in range(2):
                 for i, (r, t0, width) in enumerate(pieces(u, b)):
                     nc.scalar.activation(out=z[u][:, r, t0:t0 + width], in_=sz[u, b][:, i * width:(i + 1) * width],
-                                         func=ACT.Sigmoid, bias=bias["z"][:, u // CHUNKS, r:r + 1])
+                                         func=ACT.Sigmoid, bias=bias["z"][:, u % 2, r:r + 1])
 
         def gated(u, b):
             if b == 0:
@@ -211,20 +211,21 @@ def tile_mix_gru_mgu_kernel(
             for b in range(2):
                 for r, t0, width in pieces(u, b):
                     nc.scalar.activation(out=cand[u][:, r, t0:t0 + width], in_=y[u][:, r, t0:t0 + width],
-                                         func=ACT.Tanh, bias=bias["n"][:, u // CHUNKS, r:r + 1])
+                                         func=ACT.Tanh, bias=bias["n"][:, u % 2, r:r + 1])
 
-        def step(u):
+        def blend(eng, out, u, view, other, op):
+            eng.tensor_tensor(out=view(out), in0=view(cand[u]), in1=view(other), op=op)
+
+        def halves(out, u, other, op):
             for b in range(2):
-                nc.vector.tensor_tensor(out=part(cand[u], u, b), in0=part(cand[u], u, b), in1=part(h_sb[u], u, b), op=ALU.subtract)
-            for b in range(2):
-                nc.vector.tensor_tensor(out=part(cand[u], u, b), in0=part(cand[u], u, b), in1=part(z[u], u, b), op=ALU.mult)
+                blend(nc.vector, out, u, lambda t: part(t, u, b), other, op)
 
         def store_out(u, t0, t1):
             nc.sync.dma_start(out=unit_rows(out_0, u)[:, :, t0:t1], in_=o_sb[u][:, :, t0:t1])
 
-        def store_codes(a, t0, t1):
-            nc.sync.dma_start(out=out_1[a].rearrange("p t i -> p (t i)")[:, 4 * t0:4 * t1].bitcast(I32),
-                              in_=o_codes[a][:, t0:t1].bitcast(I32))
+        def store_codes(t0, t1):
+            nc.sync.dma_start(out=out_1.rearrange("a p t i -> p a (t i)")[:, :, 4 * t0:4 * t1].bitcast(I32),
+                              in_=o_codes[:, :, t0:t1].bitcast(I32))
 
         nc.vector.memset(s_raw["z"][:].bitcast(I32), 0)
         nc.vector.memset(hq_plane[:].bitcast(I32), 0)
@@ -251,25 +252,29 @@ def tile_mix_gru_mgu_kernel(
             load_w_scales(nc.gpsimd, "n", q)
         load_bias(nc.gpsimd, "z")
         load_bias(nc.gpsimd, "n")
+        load_u("z", 1)
+        load_w("z", 1)
+        load_u("n", 1)
+        load_w("n", 1)
         load_x(1)
         load_hq(1)
-        load_u("z", 1)
         load_h(0)
         load_x(2)
-        load_hq(2)
-        load_u("n", 1)
         load_h(1)
-        load_w("z", 1)
-        load_w("n", 1)
+        load_hq(2)
+        load_h(2)
         load_x(3)
+        load_h(3)
         load_hq(3)
-        for u in range(2, UNITS):
+        for u in range(4, UNITS):
             load_h(u)
 
-        x_bf = interleave(x_raw[0][:], "x_bf")
+        x_bf = {c: None for c in range(CHUNKS)}
+        x_bf[0] = bf_tile("x_bf")
+        interleave(x_bf[0], x_raw[0], 0, W)
         deal_u("z", 0)
         deal_w("z", 0)
-        quantize_x(0, x_bf)
+        quantize_x(0, x_bf[0])
         deal_s("z", 0)
         deal_u("n", 0)
         deal_s("n", 0)
@@ -280,53 +285,78 @@ def tile_mix_gru_mgu_kernel(
         for b in range(2):
             mm_xn(0, b)
         gate(0)
-
-        later_deals = {0: [(deal_u, "z")], 1: [(deal_u, "n")], 2: [(deal_w, "z"), (deal_w, "n")]}
-        o_bf = {}
-        for u in range(UNITS):
-            nxt = u + 1
-            if nxt < CHUNKS:
-                x_bf = interleave(x_raw[nxt][:], "x_bf")
-            gated(u, 0)
-            if u == 0:
-                deal_s("z", 1)
-                deal_s("n", 1)
-            gated(u, 1)
-            preact(u)
-            if u >= 1:
-                nc.gpsimd.tensor_tensor(out=o_sb[u - 1][:], in0=cand[u - 1][:], in1=h_sb[u - 1][:], op=ALU.add)
-                store_out(u - 1, 0, W)
-            if nxt < CHUNKS:
-                quantize_x(nxt, x_bf)
-            if u >= 2:
-                quantize_o(u - 2, 0, W, o_bf[u - 2])
-                if u - 2 == CHUNKS - 1:
-                    store_codes(0, 0, T)
-                if u == UNITS - 1:
-                    store_codes(1, 0, T - 2 * W)
-            for fn, g in later_deals.get(u, []):
-                fn(g, 1)
-            candidate(u)
-            if nxt < UNITS:
-                for mm in (mm_hn, mm_sz, mm_xn):
-                    for b in range(2):
-                        mm(nxt, b)
-                gate(nxt)
-            if u >= 1:
-                o_bf[u - 1] = interleave(o_sb[u - 1][:], "o_bf")
-            step(u)
+        x_bf[1] = bf_tile("x_bf")
+        interleave(x_bf[1], x_raw[1], 0, W)
+        deal_s("z", 1)
+        gated(0, 0)
+        deal_s("n", 1)
+        gated(0, 1)
+        deal_u("z", 1)
+        deal_w("z", 1)
+        deal_u("n", 1)
+        deal_w("n", 1)
+        quantize_x(1, x_bf[1])
+        for mm in (mm_sz, mm_hn):
+            for b in range(2):
+                mm(1, b)
+        gate(1)
 
         last = UNITS - 1
-        tail = []
+        o_bf = {}
+        for u in range(last):
+            preact(u)
+            for b in range(2):
+                gated(u + 1, b)
+            if u >= 1:
+                blend(nc.gpsimd, o_sb[u - 1], u - 1, lambda t: t[:], h_sb[u - 1], ALU.add)
+                store_out(u - 1, 0, W)
+            candidate(u)
+            if u == 0:
+                x_bf[2] = bf_tile("x_bf")
+                interleave(x_bf[2], x_raw[2], 0, W)
+            if u == 1:
+                x_bf[3] = bf_tile("x_bf")
+            if u in (1, 2):
+                interleave(x_bf[3], x_raw[3], (u - 1) * HALF, u * HALF)
+            if u >= 1:
+                o_bf[u - 1] = bf_tile("o_bf")
+                interleave(o_bf[u - 1], o_sb[u - 1], 0, W)
+            for b in range(2):
+                mm_xn(u + 1, b)
+            if u + 2 < UNITS:
+                for mm in (mm_sz, mm_hn):
+                    for b in range(2):
+                        mm(u + 2, b)
+                gate(u + 2)
+            halves(cand[u], u, h_sb[u], ALU.subtract)
+            if u == 3:
+                quantize_x(3, x_bf[3])
+            halves(cand[u], u, z[u], ALU.mult)
+            if u == 0:
+                quantize_x(2, x_bf[2])
+            else:
+                quantize_o(u - 1, 0, W, o_bf[u - 1])
+            if u in (4, 6):
+                store_codes(0 if u == 4 else 2 * W, u // 2 * W)
+
+        preact(last)
+        blend(nc.gpsimd, o_sb[last - 1], last - 1, lambda t: part(t, last - 1, 0), h_sb[last - 1], ALU.add)
+        blend(nc.vector, o_sb[last - 1], last - 1, lambda t: part(t, last - 1, 1), h_sb[last - 1], ALU.add)
+        store_out(last - 1, 0, W)
+        candidate(last)
+        o_bf[last - 1] = bf_tile("o_bf")
+        interleave(o_bf[last - 1], o_sb[last - 1], 0, W)
+        halves(cand[last], last, h_sb[last], ALU.subtract)
+        halves(cand[last], last, z[last], ALU.mult)
+        halves(o_sb[last], last, h_sb[last], ALU.add)
+        o_bf[last] = bf_tile("o_bf")
         for b in range(2):
-            nc.vector.tensor_tensor(out=part(o_sb[last], last, b), in0=part(cand[last], last, b),
-                                    in1=part(h_sb[last], last, b), op=ALU.add)
-            tail.append(interleave(part(o_sb[last], last, b), "o_bf"))
+            interleave(o_bf[last], o_sb[last], b * HALF, (b + 1) * HALF)
             store_out(last, b * HALF, (b + 1) * HALF)
         quantize_o(last - 1, 0, W, o_bf[last - 1])
         for b in range(2):
-            quantize_o(last, b * HALF, HALF, tail[b])
-        store_codes(1, T - 2 * W, T)
+            quantize_o(last, b * HALF, HALF, o_bf[last])
+        store_codes(T - W, T)
         for q in range(4):
             nc.sync.dma_start(out=out_2[:, 4 * q:4 * q + 4, :].rearrange("a r t -> r a t").bitcast(I32),
                               in_=o_plane[32 * q:32 * q + 4, :, :].bitcast(I32))

from contextlib import ExitStack

import concourse.mybir as mybir

K, N, T = 512, 1024, 1024
FLOPS = 2 * T * N * (2 * K + 2 * N)

F32 = mybir.dt.float32
BF16 = mybir.dt.bfloat16
I32 = mybir.dt.int32
U32 = mybir.dt.uint32
U8 = mybir.dt.uint8
FP8X4 = mybir.dt.float8_e4m3fn_x4
FP4X4 = mybir.dt.float4_e2m1fn_x4
ACT = mybir.ActivationFunctionType
ALU = mybir.AluOpType

P = 128
PACK = 4
ROWS = P * PACK
W = 256
HALF = W // 2
CHUNKS = T // W
UNITS = (N // ROWS) * CHUNKS


def tile_mix_gru_mgu_kernel(
    tc, x, hq_words, hq_scales, wz_words, wz_scales, uz_words, uz_scales,
    wn_words, wn_scales, un_words, un_scales, bz, bn, h, out_0, out_1, out_2,
):
    nc = tc.nc
    with ExitStack() as ctx:
        keep = ctx.enter_context(tc.tile_pool(name="keep", bufs=1))
        work = ctx.enter_context(tc.tile_pool(name="work", bufs=2))
        psum = ctx.enter_context(tc.psum_pool(name="psum", bufs=2))
        ctx.enter_context(tc.manual_schedule())

        def kept(name, shape, dtype):
            return keep.tile(shape, dtype, name=name, align_bytes=64)

        x_raw = [kept("x_raw%d" % c, [P, PACK, W], F32) for c in range(CHUNKS)]
        x_codes = kept("x_codes", [P, T], U32)
        x_plane = kept("x_plane", [P, T], U8)
        hq_codes = [kept("hq_codes%d" % c, [P, 2, W], U32) for c in range(CHUNKS)]
        hq_plane = kept("hq_plane", [P, 2, T], U8)
        h_sb = [kept("h_sb%d" % u, [P, PACK, W], F32) for u in range(UNITS)]
        o_sb = [kept("o_sb%d" % u, [P, PACK, W], F32) for u in range(UNITS)]
        o_codes = kept("o_codes", [P, 2, T], U32)
        o_plane = kept("o_plane", [P, 2, T], U8)
        gates = ("z", "n")
        w_words = {"z": wz_words, "n": wn_words}
        w_scales = {"z": wz_scales, "n": wn_scales}
        u_words = {"z": uz_words, "n": un_words}
        u_scales = {"z": uz_scales, "n": un_scales}
        bias_hbm = {"z": bz, "n": bn}
        bias = {g: kept("bias_" + g, [P, 2, PACK], F32) for g in gates}
        s_raw = {g: kept("s_raw_" + g, [P, N], U8) for g in gates}
        u_raw, u_dealt, w_raw, w_dealt, s_dealt = {}, {}, {}, {}, {}
        for g in gates:
            for a in range(2):
                u_raw[g, a] = kept("u_raw_%s%d" % (g, a), [P, 2, ROWS], U32)
                u_dealt[g, a] = kept("u_dealt_%s%d" % (g, a), [P, 2, ROWS], U32)
                w_raw[g, a] = kept("w_raw_%s%d" % (g, a), [P, 2 * ROWS], U8)
                w_dealt[g, a] = kept("w_dealt_%s%d" % (g, a), [P, 2 * ROWS], U8)
                s_dealt[g, a] = kept("s_dealt_%s%d" % (g, a), [P, ROWS], U8)

        def unit_rows(ap, u):
            c, a = divmod(u, 2)
            return ap[a * ROWS:(a + 1) * ROWS, c * W:(c + 1) * W].rearrange("(p r) t -> p r t", r=PACK)

        def load_x(c):
            nc.sync.dma_start(out=x_raw[c][:], in_=x[:, c * W:(c + 1) * W].rearrange("(p j) t -> p j t", j=PACK))

        def load_hq(c):
            src = hq_words.rearrange("g p t i -> p g (t i)")[:, :, 4 * c * W:4 * (c + 1) * W]
            nc.sync.dma_start(out=hq_codes[c][:].bitcast(I32), in_=src.bitcast(I32))

        def load_u(g, a):
            src = u_words[g].rearrange("g p n i -> p g (n i)")[:, :, 4 * a * ROWS:4 * (a + 1) * ROWS]
            nc.sync.dma_start(out=u_raw[g, a][:].bitcast(I32), in_=src.bitcast(I32))

        def load_w(g, a):
            src = w_words[g][0][:, 2 * a * ROWS:2 * (a + 1) * ROWS]
            nc.sync.dma_start(out=w_raw[g, a][:].bitcast(I32), in_=src.bitcast(I32))

        def load_h(u):
            nc.sync.dma_start(out=h_sb[u][:], in_=unit_rows(h, u))

        def load_w_scales(eng, g, q):
            eng.dma_start(out=s_raw[g][32 * q:32 * q + 4, :].bitcast(I32),
                          in_=w_scales[g][0][4 * q:4 * q + 4, :].bitcast(I32))

        def load_u_scales(eng, g, q):
            eng.dma_start(out=s_raw[g][32 * q + 4:32 * q + 12, :].bitcast(I32),
                          in_=u_scales[g][:, 4 * q:4 * q + 4, :].bitcast(I32))

        def load_hq_scales(eng, q):
            eng.dma_start(out=hq_plane[32 * q:32 * q + 4, :, :].bitcast(I32),
                          in_=hq_scales[:, 4 * q:4 * q + 4, :].rearrange("g r t -> r g t").bitcast(I32))

        def load_bias(eng, g):
            eng.dma_start(out=bias[g][:], in_=bias_hbm[g].rearrange("(a p r) -> p a r", a=2, r=PACK))

        def deal_u(g, a):
            nc.vector.tensor_copy(
                out=u_dealt[g, a][:].bitcast(I32).rearrange("p g (r b i) -> p g b r i", r=PACK, i=4),
                in_=u_raw[g, a][:].bitcast(I32).rearrange("p g (b i r) -> p g b r i", r=PACK, i=4))

        def deal_w(g, a):
            nc.vector.tensor_copy(
                out=w_dealt[g, a][:].rearrange("p (r b i y) -> p b r i y", r=PACK, i=8, y=2),
                in_=w_raw[g, a][:].rearrange("p (b i r y) -> p b r i y", r=PACK, i=8, y=2))

        def deal_s(g, a):
            nc.vector.tensor_copy(
                out=s_dealt[g, a][:].rearrange("p (r b i) -> p b r i", r=PACK, i=16),
                in_=s_raw[g][:, a * ROWS:(a + 1) * ROWS].rearrange("p (b i r) -> p b r i", r=PACK, i=16))

        def bf_tile(tag):
            return work.tile([P, PACK * W], BF16, name=tag, tag=tag, bufs=3, align_bytes=64)

        def interleave(dst, src, t0, t1):
            nc.scalar.copy(
                out=dst[:, PACK * t0:PACK * t1].rearrange("p (c i j) -> p c j i", i=2, j=PACK),
                in_=src[:, :, t0:t1].rearrange("p j (c i) -> p c j i", i=2))

        def quantize(codes, plane, src):
            nc.vector.quantize_mx(out=codes.bitcast(FP8X4), scales=plane, in_=src)

        def quantize_x(c, src):
            quantize(x_codes[:, c * W:(c + 1) * W], x_plane[:, c * W:(c + 1) * W], src[:])

        def quantize_o(u, t0, width, src):
            c, a = divmod(u, 2)
            cols = slice(c * W + t0, c * W + t0 + width)
            quantize(o_codes[:, a, cols], o_plane[:, a, cols], src[:, PACK * t0:PACK * (t0 + width)])

        def pieces(u, b):
            if u == UNITS - 1:
                return [(r, b * HALF, HALF) for r in range(PACK)]
            return [(r, 0, W) for r in (2 * b, 2 * b + 1)]

        def part(tile, u, b):
            if u == UNITS - 1:
                return tile[:, :, b * HALF:(b + 1) * HALF]
            return tile[:, 2 * b:2 * b + 2, :]

        def bank_view(bank, u):
            return bank[:].rearrange("p (r t) -> p r t", t=HALF if u == UNITS - 1 else W)

        def u_pass(dst, g, u, r, t0, width, j, start, stop):
            c, a = divmod(u, 2)
            cols = slice(r * P, (r + 1) * P)
            nc.tensor.matmul_mx(
                out=dst, lhsT=u_dealt[g, a][:, j, cols].bitcast(FP8X4),
                lhsT_scale=s_dealt[g, a][4 * (j + 1):P, cols],
                rhs=hq_codes[c][:, j, t0:t0 + width].bitcast(FP8X4),
                rhs_scale=hq_plane[:, j, c * W + t0:c * W + t0 + width], start=start, stop=stop)

        def w_pass(dst, g, u, r, t0, width, start, stop):
            c, a = divmod(u, 2)
            cols = slice(c * W + t0, c * W + t0 + width)
            nc.tensor.matmul_mx(
                out=dst, lhsT=w_dealt[g, a][:, 2 * r * P:2 * (r + 1) * P].bitcast(FP4X4),
                lhsT_scale=s_dealt[g, a][:, r * P:(r + 1) * P],
                rhs=x_codes[:, cols].bitcast(FP8X4), rhs_scale=x_plane[:, cols], start=start, stop=stop)

        sz, hn, xn, z, y, cand = {}, {}, {}, {}, {}, {}

        def mm_sz(u, b):
            sz[u, b] = psum.tile([P, 512], F32, name="sz", tag="sz", bufs=3)
            todo = list(enumerate(pieces(u, b)))
            for i, (r, t0, width) in todo:
                for j in range(2):
                    u_pass(sz[u, b][:, i * width:(i + 1) * width], "z", u, r, t0, width, j, i == 0 and j == 0, False)
            for i, (r, t0, width) in todo:
                for s in range(0, width, HALF):
                    col = i * width + s
                    w_pass(sz[u, b][:, col:col + HALF], "z", u, r, t0 + s, HALF, False, col + HALF == 512)

        def mm_hn(u, b):
            hn[u, b] = psum.tile([P, 512], F32, name="hn", tag="hn", bufs=2)
            for i, (r, t0, width) in enumerate(pieces(u, b)):
                dst = hn[u, b][:, i * width:(i + 1) * width]
                u_pass(dst, "n", u, r, t0, width, 0, True, False)
                u_pass(dst, "n", u, r, t0, width, 1, False, True)

        def mm_xn(u, b):
            xn[u, b] = psum.tile([P, 512], F32, name="xn", tag="xn", bufs=3)
            for i, (r, t0, width) in enumerate(pieces(u, b)):
                w_pass(xn[u, b][:, i * width:(i + 1) * width], "n", u, r, t0, width, True, True)

        def gate(u):
            z[u] = work.tile([P, PACK, W], F32, name="z", tag="z", bufs=3)
            for b in range(2):
                for i, (r, t0, width) in enumerate(pieces(u, b)):
                    nc.scalar.activation(out=z[u][:, r, t0:t0 + width], in_=sz[u, b][:, i * width:(i + 1) * width],
                                         func=ACT.Sigmoid, bias=bias["z"][:, u % 2, r:r + 1])

        def gated(u, b):
            if b == 0:
                y[u] = work.tile([P, PACK, W], F32, name="y", tag="y", bufs=2)
            nc.vector.tensor_tensor(out=part(y[u], u, b), in0=bank_view(hn[u, b], u), in1=part(z[u], u, b), op=ALU.mult)

        def preact(u):
            for b in range(2):
                nc.vector.tensor_tensor(out=part(y[u], u, b), in0=bank_view(xn[u, b], u), in1=part(y[u], u, b), op=ALU.add)

        def candidate(u):
            cand[u] = work.tile([P, PACK, W], F32, name="cand", tag="cand", bufs=3)
            for b in range(2):
                for r, t0, width in pieces(u, b):
                    nc.scalar.activation(out=cand[u][:, r, t0:t0 + width], in_=y[u][:, r, t0:t0 + width],
                                         func=ACT.Tanh, bias=bias["n"][:, u % 2, r:r + 1])

        def blend(eng, out, u, view, other, op):
            eng.tensor_tensor(out=view(out), in0=view(cand[u]), in1=view(other), op=op)

        def halves(out, u, other, op):
            for b in range(2):
                blend(nc.vector, out, u, lambda t: part(t, u, b), other, op)

        def store_out(u, t0, t1):
            nc.sync.dma_start(out=unit_rows(out_0, u)[:, :, t0:t1], in_=o_sb[u][:, :, t0:t1])

        def store_codes(t0, t1):
            nc.sync.dma_start(out=out_1.rearrange("a p t i -> p a (t i)")[:, :, 4 * t0:4 * t1].bitcast(I32),
                              in_=o_codes[:, :, t0:t1].bitcast(I32))

        nc.vector.memset(s_raw["z"][:].bitcast(I32), 0)
        nc.vector.memset(hq_plane[:].bitcast(I32), 0)
        nc.vector.memset(s_raw["n"][:].bitcast(I32), 0)
        load_u("z", 0)
        load_x(0)
        for q in range(4):
            load_u_scales(nc.sync, "z", q)
        for q in range(2):
            load_w_scales(nc.sync, "z", q)
        load_hq(0)
        load_w("z", 0)
        for q in range(2, 4):
            load_w_scales(nc.sync, "z", q)
        for q in range(4):
            load_hq_scales(nc.sync, q)
        load_u("n", 0)
        load_w("n", 0)
        for q in range(4):
            load_u_scales(nc.sync, "n", q)
        for q in range(2):
            load_w_scales(nc.sync, "n", q)
        for q in range(2, 4):
            load_w_scales(nc.gpsimd, "n", q)
        load_bias(nc.gpsimd, "z")
        load_bias(nc.gpsimd, "n")
        load_u("z", 1)
        load_w("z", 1)
        load_u("n", 1)
        load_w("n", 1)
        load_x(1)
        load_hq(1)
        load_h(0)
        load_x(2)
        load_h(1)
        load_hq(2)
        load_h(2)
        load_x(3)
        load_h(3)
        load_hq(3)
        for u in range(4, UNITS):
            load_h(u)

        x_bf = {c: None for c in range(CHUNKS)}
        x_bf[0] = bf_tile("x_bf")
        interleave(x_bf[0], x_raw[0], 0, W)
        deal_u("z", 0)
        deal_w("z", 0)
        quantize_x(0, x_bf[0])
        deal_s("z", 0)
        deal_u("n", 0)
        deal_s("n", 0)
        deal_w("n", 0)
        for b in range(2):
            mm_sz(0, b)
            mm_hn(0, b)
        for b in range(2):
            mm_xn(0, b)
        gate(0)
        x_bf[1] = bf_tile("x_bf")
        interleave(x_bf[1], x_raw[1], 0, W)
        deal_s("z", 1)
        gated(0, 0)
        deal_s("n", 1)
        gated(0, 1)
        deal_u("z", 1)
        deal_w("z", 1)
        deal_u("n", 1)
        deal_w("n", 1)
        quantize_x(1, x_bf[1])
        for mm in (mm_sz, mm_hn):
            for b in range(2):
                mm(1, b)
        gate(1)

        last = UNITS - 1
        o_bf = {}
        for u in range(last):
            preact(u)
            for b in range(2):
                gated(u + 1, b)
            if u >= 1:
                blend(nc.gpsimd, o_sb[u - 1], u - 1, lambda t: t[:], h_sb[u - 1], ALU.add)
                store_out(u - 1, 0, W)
            candidate(u)
            if u == 0:
                x_bf[2] = bf_tile("x_bf")
                interleave(x_bf[2], x_raw[2], 0, W)
            if u == 1:
                x_bf[3] = bf_tile("x_bf")
            if u in (1, 2):
                interleave(x_bf[3], x_raw[3], (u - 1) * HALF, u * HALF)
            if u >= 1:
                o_bf[u - 1] = bf_tile("o_bf")
                interleave(o_bf[u - 1], o_sb[u - 1], 0, W)
            for b in range(2):
                mm_xn(u + 1, b)
            if u + 2 < UNITS:
                for mm in (mm_sz, mm_hn):
                    for b in range(2):
                        mm(u + 2, b)
                gate(u + 2)
            halves(cand[u], u, h_sb[u], ALU.subtract)
            if u == 3:
                quantize_x(3, x_bf[3])
            halves(cand[u], u, z[u], ALU.mult)
            if u == 0:
                quantize_x(2, x_bf[2])
            else:
                quantize_o(u - 1, 0, W, o_bf[u - 1])
            if u in (4, 6):
                store_codes(0 if u == 4 else 2 * W, u // 2 * W)

        preact(last)
        blend(nc.gpsimd, o_sb[last - 1], last - 1, lambda t: part(t, last - 1, 0), h_sb[last - 1], ALU.add)
        blend(nc.vector, o_sb[last - 1], last - 1, lambda t: part(t, last - 1, 1), h_sb[last - 1], ALU.add)
        store_out(last - 1, 0, W)
        candidate(last)
        o_bf[last - 1] = bf_tile("o_bf")
        interleave(o_bf[last - 1], o_sb[last - 1], 0, W)
        halves(cand[last], last, h_sb[last], ALU.subtract)
        halves(cand[last], last, z[last], ALU.mult)
        halves(o_sb[last], last, h_sb[last], ALU.add)
        o_bf[last] = bf_tile("o_bf")
        for b in range(2):
            interleave(o_bf[last], o_sb[last], b * HALF, (b + 1) * HALF)
            store_out(last, b * HALF, (b + 1) * HALF)
        quantize_o(last - 1, 0, W, o_bf[last - 1])
        for b in range(2):
            quantize_o(last, b * HALF, HALF, o_bf[last])
        store_codes(T - W, T)
        for q in range(4):
            nc.sync.dma_start(out=out_2[:, 4 * q:4 * q + 4, :].rearrange("a r t -> r a t").bitcast(I32),
                              in_=o_plane[32 * q:32 * q + 4, :, :].bitcast(I32))
